import numpy as np
import ml_dtypes


def mxq(x, axis, fmt="e4m3"):
    dtype, down = {"e4m3": (ml_dtypes.float8_e4m3fn, 7), "e5m2": (ml_dtypes.float8_e5m2, 14)}[fmt]
    v = np.moveaxis(np.asarray(x, np.float32).astype(ml_dtypes.bfloat16).astype(np.float64), axis, -1)
    blocks = v.reshape(v.shape[:-1] + (-1, 32))
    amax = np.abs(blocks).max(-1, keepdims=True)
    byte = np.maximum(np.where(amax > 0, np.frexp(amax)[1] - 1 + 127, 0) - down, 1)
    scale = np.exp2(byte - 127.0)
    codes = (blocks / scale).astype(np.float32).astype(dtype).astype(np.float64)
    return np.moveaxis((codes * scale).reshape(v.shape), -1, axis)


WIDE = False


def mx_kscale(k):
    if not WIDE:
        return np.ones(k)
    levels = np.array([10, -10, 5, -5, 0])
    if k % 512:
        return np.exp2(np.random.permutation(np.resize(levels, k // 32))).repeat(32)
    a = np.empty((k // 512, 16))
    for p in range(k // 512):
        a[p, :8] = np.random.permutation(np.resize(levels, 8))
        for g in range(8):
            far = levels[np.abs(levels - a[p, g]) >= 10]
            a[p, g + 8] = far[np.random.randint(len(far))]
    return np.exp2(a.ravel()).repeat(32)


def f64(x):
    return np.asarray(x).astype(np.float64)


def striped(idx):
    return np.tile(idx.reshape(-1, 16).T, (8, 1)).astype(np.uint16)


def unstriped(offs):
    return offs[:16].T.reshape(-1).astype(np.int64)


def pack_weight(w):
    k, n = w.shape
    w = f64(np.asarray(w, np.float32).astype(ml_dtypes.bfloat16)).reshape(k // 32, 32, n)
    amax = np.abs(w).max(1)
    byte = np.clip(np.where(amax > 0, np.frexp(amax)[1] - 1 + 127 - 7, 1), 1, 254)
    scaled = (w * np.exp2(127.0 - byte)[:, None, :]).reshape(k, n).astype(np.float32)
    words = np.ascontiguousarray(scaled.reshape(k // 512, 128, 4, n).transpose(0, 1, 3, 2)).astype(ml_dtypes.float8_e4m3fn).view(np.uint8)
    return words, np.ascontiguousarray(byte.astype(np.uint8).reshape(k // 512, 16, n))


def unpack_weight(words, scales):
    g, p, n, _ = words.shape
    vals = np.ascontiguousarray(words).view(ml_dtypes.float8_e4m3fn).astype(np.float64) * np.repeat(np.exp2(scales.astype(np.float64) - 127.0), 8, axis=1)[..., None]
    return vals.transpose(0, 1, 3, 2).reshape(g * 512, n)


def sigmoid(v):
    return 1.0 / (1.0 + np.exp(-np.maximum(v, -700.0)))


K, T, S, J = 1024, 2048, 512, 256


def setup_inputs():
    n = np.random.standard_normal
    s = mx_kscale(K)[:, None]
    packed_xT = pack_weight(n((K, T)) * s)
    packed_eT = pack_weight(n((K, T)) * s)
    return {
        "x_words": packed_xT[0],
        "x_scales": packed_xT[1],
        "e_words": packed_eT[0],
        "e_scales": packed_eT[1],
        "hT": (n((K, J)) / np.sqrt(K) / s).astype(np.float32),
        "gT": (n((K, J)) / np.sqrt(K) / s).astype(np.float32),
        "offs": striped(np.random.permutation(T)[:S]),
    }


def reference(x_words, x_scales, e_words, e_scales, hT, gT, offs):
    hTq = mxq(f64(hT), 0, "e4m3")
    xq = unpack_weight(x_words, x_scales)[:, unstriped(offs)]
    y = hTq.T @ xq
    e = np.exp(y - y.max(axis=1, keepdims=True))
    p = e / e.sum(axis=1, keepdims=True)
    gTq = mxq(f64(gT), 0, "e4m3")
    e_offs = unpack_weight(e_words, e_scales)[:, unstriped(offs)]
    z = gTq.T @ e_offs
    return p * sigmoid(z)

@@ -1,0 +1,150 @@
+from contextlib import ExitStack
+
+import concourse.mybir as mybir
+
+K, T, S, J = 1024, 2048, 512, 256
+FLOPS = 2 * 2 * K * S * J
+
+F32 = mybir.dt.float32
+BF16 = mybir.dt.bfloat16
+I32 = mybir.dt.int32
+U32 = mybir.dt.uint32
+U16 = mybir.dt.uint16
+U8 = mybir.dt.uint8
+FP8X4 = mybir.dt.float8_e4m3fn_x4
+ACT = mybir.ActivationFunctionType
+ALU = mybir.AluOpType
+
+P = 128
+PACK = 4
+PASSES = K // (P * PACK)
+HALF = S // 2
+
+
+def tile_picked_zesmm_soft_p_kernel(tc, x_words, x_scales, e_words, e_scales, hT, gT, offs, out):
+    nc = tc.nc
+    with ExitStack() as ctx:
+        keep = ctx.enter_context(tc.tile_pool(name="keep", bufs=1))
+        psum = ctx.enter_context(tc.psum_pool(name="psum", bufs=1))
+
+        offsets = keep.tile([P, S // 16], U16, name="offsets")
+
+        def load_scales(name, scales, first_row, memset):
+            table = keep.tile([P, T], U8, name=name, align_bytes=64)
+            memset(table[:].bitcast(I32), 0)
+            for q in range(4):
+                row = 32 * q + first_row
+                nc.gpsimd.dma_start(
+                    out=table[row : row + 4 * PASSES, :].bitcast(I32),
+                    in_=scales[:, 4 * q : 4 * q + 4, :].bitcast(I32),
+                )
+            return table
+
+        def load_words(name, words, c):
+            table = keep.tile([P, T], U32, name=name, align_bytes=64)
+            nc.sync.dma_start(out=table[:].bitcast(I32), in_=words[c].rearrange("p n t -> p (n t)").bitcast(I32))
+            return table
+
+        def load_users(name, users, c, cols):
+            width = cols.stop - cols.start
+            raw = keep.tile([P, PACK, width], F32, name=name)
+            rows = users[c * P * PACK : (c + 1) * P * PACK, cols]
+            nc.sync.dma_start(out=raw[:], in_=rows.rearrange("(p j) w -> p j w", j=PACK))
+            return raw
+
+        def interleave(name, raw, copy):
+            width = raw.shape[2]
+            grouped = keep.tile([P, width, PACK], BF16, name=name, align_bytes=64)
+            copy(
+                out=grouped[:].rearrange("p (c i) j -> p c j i", i=4),
+                in_=raw[:].rearrange("p j (c i) -> p c j i", i=4),
+            )
+            return grouped
+
+        def quantize(name, grouped):
+            width = grouped.shape[1]
+            codes = keep.tile([P, width], U32, name=name + "_codes", align_bytes=64)
+            plane = keep.tile([P, width], U8, name=name + "_plane", align_bytes=64)
+            nc.vector.quantize_mx(
+                out=codes[:].bitcast(FP8X4), scales=plane[:], in_=grouped[:].rearrange("p w j -> p (w j)")
+            )
+            return codes, plane
+
+        def gather(name, table, dtype):
+            picked = keep.tile([P, S], dtype, name=name, align_bytes=64)
+            nc.vector.tensor_copy(out=picked[:], in_=table[:].indirect(offsets[:]))
+            return picked
+
+        def product(acc, users, user_cols, words, planes, plane_row, cols, c):
+            nc.tensor.matmul_mx(
+                out=acc[:],
+                lhsT=users[0][:, user_cols].bitcast(FP8X4),
+                lhsT_scale=users[1][:, user_cols],
+                rhs=words[:, cols].bitcast(FP8X4),
+                rhs_scale=planes[plane_row:P, cols],
+                start=(c == 0),
+                stop=(c == PASSES - 1),
+            )
+
+        everyone = slice(0, J)
+        tiles = [slice(u * P, (u + 1) * P) for u in range(J // P)]
+        halves = [slice(h * HALF, (h + 1) * HALF) for h in range(2)]
+        X_ROW, E_ROW = 0, 8
+
+        x_table_scales = load_scales("x_table_scales", x_scales, X_ROW, nc.gpsimd.memset)
+        e_table_scales = load_scales("e_table_scales", e_scales, E_ROW, nc.vector.memset)
+        h_raw = [load_users("h_raw0", hT, 0, everyone)]
+        nc.sync.dma_start(offsets[:], offs)
+        h_raw.append(load_users("h_raw1", hT, 1, everyone))
+        x_table = [load_words("x_table%d" % c, x_words, c) for c in range(PASSES)]
+        e_table = [load_words("e_table0", e_words, 0)]
+        g_raw0 = load_users("g_raw0", gT, 0, everyone)
+        e_table.append(load_words("e_table1", e_words, 1))
+        g_raw1 = [load_users("g_raw1_%d" % u, gT, 1, tiles[u]) for u in range(2)]
+
+        h_q = [quantize("h%d" % c, interleave("h_grouped%d" % c, h_raw[c], nc.scalar.copy)) for c in range(PASSES)]
+        x_picked = [gather("x_picked0", x_table[0], U32)]
+        x_planes = gather("x_planes", x_table_scales, U8)
+        x_picked.append(gather("x_picked1", x_table[1], U32))
+        y = [psum.tile([P, S], F32, name="y%d" % u) for u in range(2)]
+        for c in range(PASSES):
+            for u in range(2):
+                product(y[u], h_q[c], tiles[u], x_picked[c], x_planes, X_ROW + 4 * c, slice(0, S), c)
+
+        expy, inv, total = [], [], []
+        for u in range(2):
+            neg_max = keep.tile([P, 1], F32, name="neg_max%d" % u)
+            nc.vector.tensor_reduce(out=neg_max[:], in_=y[u][:], axis=mybir.AxisListType.X, op=ALU.max, negate=True)
+            expy.append(keep.tile([P, S], F32, name="expy%d" % u))
+            total.append(keep.tile([P, 1], F32, name="total%d" % u))
+            nc.scalar.activation(
+                out=expy[u][:], in_=y[u][:], func=ACT.Exp, bias=neg_max[:], scale=1.0, accum_out=total[u][:]
+            )
+        warm = keep.tile([P, 1], F32, name="warm")
+        nc.scalar.activation(out=warm[:], in_=total[1][:], func=ACT.Sigmoid)
+
+        z = [[psum.tile([P, HALF], F32, name="z%d%d" % (u, h)) for h in range(2)] for u in range(2)]
+        e_picked0 = gather("e_picked0", e_table[0], U32)
+        for u in range(2):
+            inv.append(keep.tile([P, 1], F32, name="inv%d" % u))
+            nc.vector.reciprocal(out=inv[u][:], in_=total[u][:])
+        e_planes = gather("e_planes", e_table_scales, U8)
+        g_q0 = quantize("g0", interleave("g_grouped0", g_raw0, nc.scalar.copy))
+        for u in range(2):
+            for h in range(2):
+                product(z[u][h], g_q0, tiles[u], e_picked0, e_planes, E_ROW, halves[h], 0)
+        e_picked1 = gather("e_picked1", e_table[1], U32)
+        copies = [nc.scalar.copy, nc.vector.tensor_copy]
+        for u in range(2):
+            g_q1 = quantize("g1_%d" % u, interleave("g_grouped1_%d" % u, g_raw1[u], copies[u]))
+            for h in range(2):
+                product(z[u][h], g_q1, slice(0, P), e_picked1, e_planes, E_ROW + 4, halves[h], 1)
+        for u in range(2):
+            for h in range(2):
+                gate = keep.tile([P, HALF], F32, name="gate%d%d" % (u, h))
+                nc.scalar.activation(out=gate[:], in_=z[u][h][:], func=ACT.Sigmoid)
+                result = keep.tile([P, HALF], F32, name="result%d%d" % (u, h))
+                nc.vector.scalar_tensor_tensor(
+                    out=result[:], in0=expy[u][:, halves[h]], scalar=inv[u][:], in1=gate[:], op0=ALU.mult, op1=ALU.mult
+                )
+                nc.sync.dma_start(out=out[tiles[u], halves[h]], in_=result[:])

@@ -29,16 +29,18 @@ def tile_picked_zesmm_soft_p_kernel(tc, x_words, x_scales, e_words, e_scales, hT
 
         offsets = keep.tile([P, S // 16], U16, name="offsets")
 
-        def load_scales(name, scales, first_row, memset):
+        def cleared(name):
             table = keep.tile([P, T], U8, name=name, align_bytes=64)
-            memset(table[:].bitcast(I32), 0)
+            nc.vector.memset(table[:].bitcast(I32), 0)
+            return table
+
+        def load_scales(table, scales, first_row):
             for q in range(4):
                 row = 32 * q + first_row
-                nc.gpsimd.dma_start(
+                nc.sync.dma_start(
                     out=table[row : row + 4 * PASSES, :].bitcast(I32),
                     in_=scales[:, 4 * q : 4 * q + 4, :].bitcast(I32),
                 )
-            return table
 
         def load_words(name, words, c):
             table = keep.tile([P, T], U32, name=name, align_bytes=64)
@@ -70,18 +72,19 @@ def tile_picked_zesmm_soft_p_kernel(tc, x_words, x_scales, e_words, e_scales, hT
             )
             return codes, plane
 
-        def gather(name, table, dtype):
-            picked = keep.tile([P, S], dtype, name=name, align_bytes=64)
-            nc.vector.tensor_copy(out=picked[:], in_=table[:].indirect(offsets[:]))
+        def gather(name, table, dtype, entries=slice(0, S)):
+            picked = keep.tile([P, entries.stop - entries.start], dtype, name=name, align_bytes=64)
+            part = offsets[:, entries.start // 16 : entries.stop // 16]
+            nc.vector.tensor_copy(out=picked[:], in_=table[:].indirect(part))
             return picked
 
-        def product(acc, users, user_cols, words, planes, plane_row, cols, c):
+        def product(acc, users, user_cols, words, planes, c):
             nc.tensor.matmul_mx(
                 out=acc[:],
                 lhsT=users[0][:, user_cols].bitcast(FP8X4),
                 lhsT_scale=users[1][:, user_cols],
-                rhs=words[:, cols].bitcast(FP8X4),
-                rhs_scale=planes[plane_row:P, cols],
+                rhs=words.bitcast(FP8X4),
+                rhs_scale=planes,
                 start=(c == 0),
                 stop=(c == PASSES - 1),
             )
@@ -91,25 +94,28 @@ def tile_picked_zesmm_soft_p_kernel(tc, x_words, x_scales, e_words, e_scales, hT
         halves = [slice(h * HALF, (h + 1) * HALF) for h in range(2)]
         X_ROW, E_ROW = 0, 8
 
-        x_table_scales = load_scales("x_table_scales", x_scales, X_ROW, nc.gpsimd.memset)
-        e_table_scales = load_scales("e_table_scales", e_scales, E_ROW, nc.vector.memset)
+        x_table_scales = cleared("x_table_scales")
+        e_table_scales = cleared("e_table_scales")
         h_raw = [load_users("h_raw0", hT, 0, everyone)]
+        load_scales(x_table_scales, x_scales, X_ROW)
         nc.sync.dma_start(offsets[:], offs)
         h_raw.append(load_users("h_raw1", hT, 1, everyone))
-        x_table = [load_words("x_table%d" % c, x_words, c) for c in range(PASSES)]
+        x_table = [load_words("x_table0", x_words, 0)]
+        load_scales(e_table_scales, e_scales, E_ROW)
+        x_table.append(load_words("x_table1", x_words, 1))
         e_table = [load_words("e_table0", e_words, 0)]
-        g_raw0 = load_users("g_raw0", gT, 0, everyone)
+        g_raw = [load_users("g_raw%d" % c, gT, c, everyone) for c in range(PASSES)]
         e_table.append(load_words("e_table1", e_words, 1))
-        g_raw1 = [load_users("g_raw1_%d" % u, gT, 1, tiles[u]) for u in range(2)]
 
         h_q = [quantize("h%d" % c, interleave("h_grouped%d" % c, h_raw[c], nc.scalar.copy)) for c in range(PASSES)]
-        x_picked = [gather("x_picked0", x_table[0], U32)]
         x_planes = gather("x_planes", x_table_scales, U8)
+        x_picked = [gather("x_picked0", x_table[0], U32)]
+        e_planes = gather("e_planes", e_table_scales, U8)
         x_picked.append(gather("x_picked1", x_table[1], U32))
         y = [psum.tile([P, S], F32, name="y%d" % u) for u in range(2)]
         for c in range(PASSES):
             for u in range(2):
-                product(y[u], h_q[c], tiles[u], x_picked[c], x_planes, X_ROW + 4 * c, slice(0, S), c)
+                product(y[u], h_q[c], tiles[u], x_picked[c][:], x_planes[X_ROW + 4 * c : P, :], c)
 
         expy, inv, total = [], [], []
         for u in range(2):
@@ -120,30 +126,26 @@ def tile_picked_zesmm_soft_p_kernel(tc, x_words, x_scales, e_words, e_scales, hT
             nc.scalar.activation(
                 out=expy[u][:], in_=y[u][:], func=ACT.Exp, bias=neg_max[:], scale=1.0, accum_out=total[u][:]
             )
-        warm = keep.tile([P, 1], F32, name="warm")
-        nc.scalar.activation(out=warm[:], in_=total[1][:], func=ACT.Sigmoid)
 
-        z = [[psum.tile([P, HALF], F32, name="z%d%d" % (u, h)) for h in range(2)] for u in range(2)]
+        z = [[psum.tile([P, HALF], F32, name="z%d%d" % (h, u)) for u in range(2)] for h in range(2)]
         e_picked0 = gather("e_picked0", e_table[0], U32)
         for u in range(2):
             inv.append(keep.tile([P, 1], F32, name="inv%d" % u))
             nc.vector.reciprocal(out=inv[u][:], in_=total[u][:])
-        e_planes = gather("e_planes", e_table_scales, U8)
-        g_q0 = quantize("g0", interleave("g_grouped0", g_raw0, nc.scalar.copy))
-        for u in range(2):
-            for h in range(2):
-                product(z[u][h], g_q0, tiles[u], e_picked0, e_planes, E_ROW, halves[h], 0)
-        e_picked1 = gather("e_picked1", e_table[1], U32)
         copies = [nc.scalar.copy, nc.vector.tensor_copy]
-        for u in range(2):
-            g_q1 = quantize("g1_%d" % u, interleave("g_grouped1_%d" % u, g_raw1[u], copies[u]))
-            for h in range(2):
-                product(z[u][h], g_q1, slice(0, P), e_picked1, e_planes, E_ROW + 4, halves[h], 1)
-        for u in range(2):
-            for h in range(2):
-                gate = keep.tile([P, HALF], F32, name="gate%d%d" % (u, h))
-                nc.scalar.activation(out=gate[:], in_=z[u][h][:], func=ACT.Sigmoid)
-                result = keep.tile([P, HALF], F32, name="result%d%d" % (u, h))
+        g_q = [quantize("g%d" % c, interleave("g_grouped%d" % c, g_raw[c], copies[c])) for c in range(PASSES)]
+        for h in range(2):
+            for u in range(2):
+                product(z[h][u], g_q[0], tiles[u], e_picked0[:, halves[h]], e_planes[E_ROW:P, halves[h]], 0)
+        for h in range(2):
+            e_picked1 = gather("e_picked1_%d" % h, e_table[1], U32, halves[h])
+            for u in range(2):
+                product(z[h][u], g_q[1], tiles[u], e_picked1[:], e_planes[E_ROW + 4 : P, halves[h]], 1)
+        for h in range(2):
+            for u in range(2):
+                gate = keep.tile([P, HALF], F32, name="gate%d%d" % (h, u))
+                nc.scalar.activation(out=gate[:], in_=z[h][u][:], func=ACT.Sigmoid)
+                result = keep.tile([P, HALF], F32, name="result%d%d" % (h, u))
                 nc.vector.scalar_tensor_tensor(
                     out=result[:], in0=expy[u][:, halves[h]], scalar=inv[u][:], in1=gate[:], op0=ALU.mult, op1=ALU.mult
                 )

@@ -29,34 +29,34 @@ def tile_picked_zesmm_soft_p_kernel(tc, x_words, x_scales, e_words, e_scales, hT
 
         offsets = keep.tile([P, S // 16], U16, name="offsets")
 
-        def cleared(name):
+        def cleared(name, engine):
             table = keep.tile([P, T], U8, name=name, align_bytes=64)
-            nc.vector.memset(table[:].bitcast(I32), 0)
+            engine.memset(table[:].bitcast(I32), 0)
             return table
 
-        def load_scales(table, scales, first_row):
+        def load_scales(table, scales, first_row, queue):
             for q in range(4):
                 row = 32 * q + first_row
-                nc.sync.dma_start(
+                queue.dma_start(
                     out=table[row : row + 4 * PASSES, :].bitcast(I32),
                     in_=scales[:, 4 * q : 4 * q + 4, :].bitcast(I32),
                 )
 
         def load_words(name, words, c):
-            table = keep.tile([P, T], U32, name=name, align_bytes=64)
+            table = keep.tile([P, T], U32, name=name, tag=name, align_bytes=64)
             nc.sync.dma_start(out=table[:].bitcast(I32), in_=words[c].rearrange("p n t -> p (n t)").bitcast(I32))
             return table
 
         def load_users(name, users, c, cols):
             width = cols.stop - cols.start
-            raw = keep.tile([P, PACK, width], F32, name=name)
+            raw = keep.tile([P, PACK, width], F32, name=name, tag=name)
             rows = users[c * P * PACK : (c + 1) * P * PACK, cols]
             nc.sync.dma_start(out=raw[:], in_=rows.rearrange("(p j) w -> p j w", j=PACK))
             return raw
 
         def interleave(name, raw, copy):
             width = raw.shape[2]
-            grouped = keep.tile([P, width, PACK], BF16, name=name, align_bytes=64)
+            grouped = keep.tile([P, width, PACK], BF16, name=name, tag=name, align_bytes=64)
             copy(
                 out=grouped[:].rearrange("p (c i) j -> p c j i", i=4),
                 in_=raw[:].rearrange("p j (c i) -> p c j i", i=4),
@@ -72,10 +72,10 @@ def tile_picked_zesmm_soft_p_kernel(tc, x_words, x_scales, e_words, e_scales, hT
             )
             return codes, plane
 
-        def gather(name, table, dtype, entries=slice(0, S)):
-            picked = keep.tile([P, entries.stop - entries.start], dtype, name=name, align_bytes=64)
+        def gather(name, table, dtype, entries=slice(0, S), slot=None):
+            picked = keep.tile([P, entries.stop - entries.start], dtype, name=name, tag=slot or name, align_bytes=64)
             part = offsets[:, entries.start // 16 : entries.stop // 16]
-            nc.vector.tensor_copy(out=picked[:], in_=table[:].indirect(part))
+            nc.vector.tensor_copy(out=picked[:], in_=table.indirect(part))
             return picked
 
         def product(acc, users, user_cols, words, planes, c):
@@ -94,51 +94,50 @@ def tile_picked_zesmm_soft_p_kernel(tc, x_words, x_scales, e_words, e_scales, hT
         halves = [slice(h * HALF, (h + 1) * HALF) for h in range(2)]
         X_ROW, E_ROW = 0, 8
 
-        x_table_scales = cleared("x_table_scales")
-        e_table_scales = cleared("e_table_scales")
+        x_table_scales = cleared("x_table_scales", nc.vector)
+        e_table_scales = cleared("e_table_scales", nc.gpsimd)
         h_raw = [load_users("h_raw0", hT, 0, everyone)]
-        load_scales(x_table_scales, x_scales, X_ROW)
+        load_scales(x_table_scales, x_scales, X_ROW, nc.sync)
         nc.sync.dma_start(offsets[:], offs)
         h_raw.append(load_users("h_raw1", hT, 1, everyone))
         x_table = [load_words("x_table0", x_words, 0)]
-        load_scales(e_table_scales, e_scales, E_ROW)
+        load_scales(e_table_scales, e_scales, E_ROW, nc.gpsimd)
         x_table.append(load_words("x_table1", x_words, 1))
-        e_table = [load_words("e_table0", e_words, 0)]
         g_raw = [load_users("g_raw%d" % c, gT, c, everyone) for c in range(PASSES)]
-        e_table.append(load_words("e_table1", e_words, 1))
+        e_table = [load_words("e_table%d" % c, e_words, c) for c in range(PASSES)]
 
         h_q = [quantize("h%d" % c, interleave("h_grouped%d" % c, h_raw[c], nc.scalar.copy)) for c in range(PASSES)]
-        x_planes = gather("x_planes", x_table_scales, U8)
-        x_picked = [gather("x_picked0", x_table[0], U32)]
-        e_planes = gather("e_planes", e_table_scales, U8)
-        x_picked.append(gather("x_picked1", x_table[1], U32))
+        x_planes = gather("x_planes", x_table_scales[:], U8)
+        x_picked = [gather("x_picked%d" % c, x_table[c][:], U32) for c in range(PASSES)]
         y = [psum.tile([P, S], F32, name="y%d" % u) for u in range(2)]
         for c in range(PASSES):
             for u in range(2):
                 product(y[u], h_q[c], tiles[u], x_picked[c][:], x_planes[X_ROW + 4 * c : P, :], c)
 
+        g_grouped = [interleave("g_grouped%d" % c, g_raw[c], nc.scalar.copy) for c in range(PASSES)]
         expy, inv, total = [], [], []
         for u in range(2):
             neg_max = keep.tile([P, 1], F32, name="neg_max%d" % u)
             nc.vector.tensor_reduce(out=neg_max[:], in_=y[u][:], axis=mybir.AxisListType.X, op=ALU.max, negate=True)
-            expy.append(keep.tile([P, S], F32, name="expy%d" % u))
+            expy.append(keep.tile([P, S], F32, name="expy%d" % u, tag="g_raw%d" % (1 - u)))
             total.append(keep.tile([P, 1], F32, name="total%d" % u))
             nc.scalar.activation(
                 out=expy[u][:], in_=y[u][:], func=ACT.Exp, bias=neg_max[:], scale=1.0, accum_out=total[u][:]
             )
 
         z = [[psum.tile([P, HALF], F32, name="z%d%d" % (h, u)) for u in range(2)] for h in range(2)]
-        e_picked0 = gather("e_picked0", e_table[0], U32)
+        g_q = [quantize("g%d" % c, g_grouped[c]) for c in range(PASSES)]
+        e_planes = gather("e_planes", e_table_scales[:], U8, slot="g_grouped1")
+        e_picked0 = gather("e_picked0", e_table[0][:], U32)
+        inverses = keep.tile([P, 16], F32, name="inverses", tag="e_table0", align_bytes=64)
         for u in range(2):
-            inv.append(keep.tile([P, 1], F32, name="inv%d" % u))
-            nc.vector.reciprocal(out=inv[u][:], in_=total[u][:])
-        copies = [nc.scalar.copy, nc.vector.tensor_copy]
-        g_q = [quantize("g%d" % c, interleave("g_grouped%d" % c, g_raw[c], copies[c])) for c in range(PASSES)]
+            inv.append(inverses[:, 8 * u : 8 * u + 1])
+            nc.vector.reciprocal(out=inv[u], in_=total[u][:])
         for h in range(2):
             for u in range(2):
                 product(z[h][u], g_q[0], tiles[u], e_picked0[:, halves[h]], e_planes[E_ROW:P, halves[h]], 0)
         for h in range(2):
-            e_picked1 = gather("e_picked1_%d" % h, e_table[1], U32, halves[h])
+            e_picked1 = gather("e_picked1_%d" % h, e_table[1][:], U32, halves[h])
             for u in range(2):
                 product(z[h][u], g_q[1], tiles[u], e_picked1[:], e_planes[E_ROW + 4 : P, halves[h]], 1)
         for h in range(2):
@@ -147,6 +146,6 @@ def tile_picked_zesmm_soft_p_kernel(tc, x_words, x_scales, e_words, e_scales, hT
                 nc.scalar.activation(out=gate[:], in_=z[h][u][:], func=ACT.Sigmoid)
                 result = keep.tile([P, HALF], F32, name="result%d%d" % (h, u))
                 nc.vector.scalar_tensor_tensor(
-                    out=result[:], in0=expy[u][:, halves[h]], scalar=inv[u][:], in1=gate[:], op0=ALU.mult, op1=ALU.mult
+                    out=result[:], in0=expy[u][:, halves[h]], scalar=inv[u], in1=gate[:], op0=ALU.mult, op1=ALU.mult
                 )
                 nc.sync.dma_start(out=out[tiles[u], halves[h]], in_=result[:])

@@ -30,26 +30,26 @@ def tile_picked_zesmm_soft_p_kernel(tc, x_words, x_scales, e_words, e_scales, hT
         offsets = keep.tile([P, S // 16], U16, name="offsets")
 
         def cleared(name, engine):
-            table = keep.tile([P, T], U8, name=name, align_bytes=64)
+            table = keep.tile([P, T], U8, name=name, tag=name, align_bytes=64)
             engine.memset(table[:].bitcast(I32), 0)
             return table
 
-        def load_scales(table, scales, first_row, queue):
+        def load_scales(table, scales, first_row, queues):
             for q in range(4):
                 row = 32 * q + first_row
-                queue.dma_start(
+                queues[q].dma_start(
                     out=table[row : row + 4 * PASSES, :].bitcast(I32),
                     in_=scales[:, 4 * q : 4 * q + 4, :].bitcast(I32),
                 )
 
-        def load_words(name, words, c):
-            table = keep.tile([P, T], U32, name=name, tag=name, align_bytes=64)
+        def load_words(name, words, c, slot=None):
+            table = keep.tile([P, T], U32, name=name, tag=slot or name, align_bytes=64)
             nc.sync.dma_start(out=table[:].bitcast(I32), in_=words[c].rearrange("p n t -> p (n t)").bitcast(I32))
             return table
 
         def load_users(name, users, c, cols):
             width = cols.stop - cols.start
-            raw = keep.tile([P, PACK, width], F32, name=name, tag=name)
+            raw = keep.tile([P, PACK, width], F32, name=name, tag=name, align_bytes=64)
             rows = users[c * P * PACK : (c + 1) * P * PACK, cols]
             nc.sync.dma_start(out=raw[:], in_=rows.rearrange("(p j) w -> p j w", j=PACK))
             return raw
@@ -95,19 +95,18 @@ def tile_picked_zesmm_soft_p_kernel(tc, x_words, x_scales, e_words, e_scales, hT
         X_ROW, E_ROW = 0, 8
 
         x_table_scales = cleared("x_table_scales", nc.vector)
-        e_table_scales = cleared("e_table_scales", nc.gpsimd)
+        e_table_scales = cleared("e_table_scales", nc.vector)
         h_raw = [load_users("h_raw0", hT, 0, everyone)]
-        load_scales(x_table_scales, x_scales, X_ROW, nc.sync)
+        load_scales(x_table_scales, x_scales, X_ROW, [nc.sync, nc.sync, nc.gpsimd, nc.gpsimd])
+        load_scales(e_table_scales, e_scales, E_ROW, [nc.gpsimd] * 4)
         nc.sync.dma_start(offsets[:], offs)
         h_raw.append(load_users("h_raw1", hT, 1, everyone))
         x_table = [load_words("x_table0", x_words, 0)]
-        load_scales(e_table_scales, e_scales, E_ROW, nc.gpsimd)
-        x_table.append(load_words("x_table1", x_words, 1))
-        g_raw = [load_users("g_raw%d" % c, gT, c, everyone) for c in range(PASSES)]
-        e_table = [load_words("e_table%d" % c, e_words, c) for c in range(PASSES)]
-
         h_q = [quantize("h%d" % c, interleave("h_grouped%d" % c, h_raw[c], nc.scalar.copy)) for c in range(PASSES)]
+        x_table.append(load_words("x_table1", x_words, 1, slot="h_raw0"))
+        g_raw = [load_users("g_raw%d" % c, gT, c, everyone) for c in range(PASSES)]
         x_planes = gather("x_planes", x_table_scales[:], U8)
+        e_table = [load_words("e_table0", e_words, 0, slot="x_table_scales"), load_words("e_table1", e_words, 1)]
         x_picked = [gather("x_picked%d" % c, x_table[c][:], U32) for c in range(PASSES)]
         y = [psum.tile([P, S], F32, name="y%d" % u) for u in range(2)]
         for c in range(PASSES):
@@ -119,7 +118,7 @@ def tile_picked_zesmm_soft_p_kernel(tc, x_words, x_scales, e_words, e_scales, hT
         for u in range(2):
             neg_max = keep.tile([P, 1], F32, name="neg_max%d" % u)
             nc.vector.tensor_reduce(out=neg_max[:], in_=y[u][:], axis=mybir.AxisListType.X, op=ALU.max, negate=True)
-            expy.append(keep.tile([P, S], F32, name="expy%d" % u, tag="g_raw%d" % (1 - u)))
+            expy.append(keep.tile([P, S], F32, name="expy%d" % u, tag="g_raw%d" % (1 - u), align_bytes=64))
             total.append(keep.tile([P, 1], F32, name="total%d" % u))
             nc.scalar.activation(
                 out=expy[u][:], in_=y[u][:], func=ACT.Exp, bias=neg_max[:], scale=1.0, accum_out=total[u][:]
@@ -127,9 +126,9 @@ def tile_picked_zesmm_soft_p_kernel(tc, x_words, x_scales, e_words, e_scales, hT
 
         z = [[psum.tile([P, HALF], F32, name="z%d%d" % (h, u)) for u in range(2)] for h in range(2)]
         g_q = [quantize("g%d" % c, g_grouped[c]) for c in range(PASSES)]
-        e_planes = gather("e_planes", e_table_scales[:], U8, slot="g_grouped1")
+        e_planes = gather("e_planes", e_table_scales[:], U8, slot="g_grouped0")
         e_picked0 = gather("e_picked0", e_table[0][:], U32)
-        inverses = keep.tile([P, 16], F32, name="inverses", tag="e_table0", align_bytes=64)
+        inverses = keep.tile([P, 16], F32, name="inverses", tag="x_table_scales", align_bytes=64)
         for u in range(2):
             inv.append(inverses[:, 8 * u : 8 * u + 1])
             nc.vector.reciprocal(out=inv[u], in_=total[u][:])

from contextlib import ExitStack

import concourse.mybir as mybir

K, T, S, J = 1024, 2048, 512, 256
FLOPS = 2 * 2 * K * S * J

F32 = mybir.dt.float32
BF16 = mybir.dt.bfloat16
I32 = mybir.dt.int32
U32 = mybir.dt.uint32
U16 = mybir.dt.uint16
U8 = mybir.dt.uint8
FP8X4 = mybir.dt.float8_e4m3fn_x4
ACT = mybir.ActivationFunctionType
ALU = mybir.AluOpType

P = 128
PACK = 4
PASSES = K // (P * PACK)
HALF = S // 2


def tile_picked_zesmm_soft_p_kernel(tc, x_words, x_scales, e_words, e_scales, hT, gT, offs, out):
    nc = tc.nc
    with ExitStack() as ctx:
        keep = ctx.enter_context(tc.tile_pool(name="keep", bufs=1))
        psum = ctx.enter_context(tc.psum_pool(name="psum", bufs=1))

        offsets = keep.tile([P, S // 16], U16, name="offsets")

        def cleared(name, engine):
            table = keep.tile([P, T], U8, name=name, tag=name, align_bytes=64)
            engine.memset(table[:].bitcast(I32), 0)
            return table

        def load_scales(table, scales, first_row, queues):
            for q in range(4):
                row = 32 * q + first_row
                queues[q].dma_start(
                    out=table[row : row + 4 * PASSES, :].bitcast(I32),
                    in_=scales[:, 4 * q : 4 * q + 4, :].bitcast(I32),
                )

        def load_words(name, words, c, slot=None):
            table = keep.tile([P, T], U32, name=name, tag=slot or name, align_bytes=64)
            nc.sync.dma_start(out=table[:].bitcast(I32), in_=words[c].rearrange("p n t -> p (n t)").bitcast(I32))
            return table

        def load_users(name, users, c, cols):
            width = cols.stop - cols.start
            raw = keep.tile([P, PACK, width], F32, name=name, tag=name, align_bytes=64)
            rows = users[c * P * PACK : (c + 1) * P * PACK, cols]
            nc.sync.dma_start(out=raw[:], in_=rows.rearrange("(p j) w -> p j w", j=PACK))
            return raw

        def interleave(name, raw, copy):
            width = raw.shape[2]
            grouped = keep.tile([P, width, PACK], BF16, name=name, tag=name, align_bytes=64)
            copy(
                out=grouped[:].rearrange("p (c i) j -> p c j i", i=4),
                in_=raw[:].rearrange("p j (c i) -> p c j i", i=4),
            )
            return grouped

        def quantize(name, grouped):
            width = grouped.shape[1]
            codes = keep.tile([P, width], U32, name=name + "_codes", align_bytes=64)
            plane = keep.tile([P, width], U8, name=name + "_plane", align_bytes=64)
            nc.vector.quantize_mx(
                out=codes[:].bitcast(FP8X4), scales=plane[:], in_=grouped[:].rearrange("p w j -> p (w j)")
            )
            return codes, plane

        def gather(name, table, dtype, entries=slice(0, S), slot=None):
            picked = keep.tile([P, entries.stop - entries.start], dtype, name=name, tag=slot or name, align_bytes=64)
            part = offsets[:, entries.start // 16 : entries.stop // 16]
            nc.vector.tensor_copy(out=picked[:], in_=table.indirect(part))
            return picked

        def product(acc, users, user_cols, words, planes, c):
            nc.tensor.matmul_mx(
                out=acc[:],
                lhsT=users[0][:, user_cols].bitcast(FP8X4),
                lhsT_scale=users[1][:, user_cols],
                rhs=words.bitcast(FP8X4),
                rhs_scale=planes,
                start=(c == 0),
                stop=(c == PASSES - 1),
            )

        everyone = slice(0, J)
        tiles = [slice(u * P, (u + 1) * P) for u in range(J // P)]
        halves = [slice(h * HALF, (h + 1) * HALF) for h in range(2)]
        X_ROW, E_ROW = 0, 8

        x_table_scales = cleared("x_table_scales", nc.vector)
        e_table_scales = cleared("e_table_scales", nc.vector)
        h_raw = [load_users("h_raw0", hT, 0, everyone)]
        load_scales(x_table_scales, x_scales, X_ROW, [nc.sync, nc.sync, nc.gpsimd, nc.gpsimd])
        load_scales(e_table_scales, e_scales, E_ROW, [nc.gpsimd] * 4)
        nc.sync.dma_start(offsets[:], offs)
        h_raw.append(load_users("h_raw1", hT, 1, everyone))
        x_table = [load_words("x_table0", x_words, 0)]
        h_q = [quantize("h%d" % c, interleave("h_grouped%d" % c, h_raw[c], nc.scalar.copy)) for c in range(PASSES)]
        x_table.append(load_words("x_table1", x_words, 1, slot="h_raw0"))
        g_raw = [load_users("g_raw%d" % c, gT, c, everyone) for c in range(PASSES)]
        x_planes = gather("x_planes", x_table_scales[:], U8)
        e_table = [load_words("e_table0", e_words, 0, slot="x_table_scales"), load_words("e_table1", e_words, 1)]
        x_picked = [gather("x_picked%d" % c, x_table[c][:], U32) for c in range(PASSES)]
        y = [psum.tile([P, S], F32, name="y%d" % u) for u in range(2)]
        for c in range(PASSES):
            for u in range(2):
                product(y[u], h_q[c], tiles[u], x_picked[c][:], x_planes[X_ROW + 4 * c : P, :], c)

        g_grouped = [interleave("g_grouped%d" % c, g_raw[c], nc.scalar.copy) for c in range(PASSES)]
        expy, inv, total = [], [], []
        for u in range(2):
            neg_max = keep.tile([P, 1], F32, name="neg_max%d" % u)
            nc.vector.tensor_reduce(out=neg_max[:], in_=y[u][:], axis=mybir.AxisListType.X, op=ALU.max, negate=True)
            expy.append(keep.tile([P, S], F32, name="expy%d" % u, tag="g_raw%d" % (1 - u), align_bytes=64))
            total.append(keep.tile([P, 1], F32, name="total%d" % u))
            nc.scalar.activation(
                out=expy[u][:], in_=y[u][:], func=ACT.Exp, bias=neg_max[:], scale=1.0, accum_out=total[u][:]
            )

        z = [[psum.tile([P, HALF], F32, name="z%d%d" % (h, u)) for u in range(2)] for h in range(2)]
        g_q = [quantize("g%d" % c, g_grouped[c]) for c in range(PASSES)]
        e_planes = gather("e_planes", e_table_scales[:], U8, slot="g_grouped0")
        e_picked0 = gather("e_picked0", e_table[0][:], U32)
        inverses = keep.tile([P, 16], F32, name="inverses", tag="x_table_scales", align_bytes=64)
        for u in range(2):
            inv.append(inverses[:, 8 * u : 8 * u + 1])
            nc.vector.reciprocal(out=inv[u], in_=total[u][:])
        for h in range(2):
            for u in range(2):
                product(z[h][u], g_q[0], tiles[u], e_picked0[:, halves[h]], e_planes[E_ROW:P, halves[h]], 0)
        for h in range(2):
            e_picked1 = gather("e_picked1_%d" % h, e_table[1][:], U32, halves[h])
            for u in range(2):
                product(z[h][u], g_q[1], tiles[u], e_picked1[:], e_planes[E_ROW + 4 : P, halves[h]], 1)
        for h in range(2):
            for u in range(2):
                gate = keep.tile([P, HALF], F32, name="gate%d%d" % (h, u))
                nc.scalar.activation(out=gate[:], in_=z[h][u][:], func=ACT.Sigmoid)
                result = keep.tile([P, HALF], F32, name="result%d%d" % (h, u))
                nc.vector.scalar_tensor_tensor(
                    out=result[:], in0=expy[u][:, halves[h]], scalar=inv[u], in1=gate[:], op0=ALU.mult, op1=ALU.mult
                )
                nc.sync.dma_start(out=out[tiles[u], halves[h]], in_=result[:])
